import numpy as np, ml_dtypes
CORES = [16,18,20,22]
N = 4
BF = ml_dtypes.bfloat16
def gentries(a):
    return np.ascontiguousarray(a.reshape(8, 16, -1).transpose(0, 2, 1)).reshape(8, -1)
def gtable(e):
    e = np.asarray(e); return np.ascontiguousarray(e.reshape(8, -1, 16).transpose(0, 2, 1)).reshape(128, -1).astype(np.int32)
R, F, C, D, B = 8192, 4096, 1536, 2, 1 << 20
def passing(at, lim):
    a0 = at[:, 0].reshape(8, R); l = lim.reshape(8, 2)
    return (a0 >= l[:, :1]) & (a0 <= l[:, 1:])
def dims(rng, m, w, first=None):
    lo = rng.integers(-(B >> 1), B >> 2, (8, 1)); hi = lo + w[:, None]; z = rng.random((8, R))
    if first is not None: z[np.arange(8), first] = -1
    ok = np.argsort(np.argsort(z, 1), 1) < m[:, None]
    out = np.where(rng.random((8, R)) < 0.5, rng.integers(1 - B, lo, (8, R)), rng.integers(hi + 1, B, (8, R)))
    return lo, hi, ok, np.where(ok, rng.integers(lo, hi + 1, (8, R)), out)
def living(n, z):
    return np.argsort(np.argsort(z, 1), 1) < n[:, None]
def facts(rng, ok, live, p, where, e=1):
    m = np.sum(ok, axis=1)[:, None]; o = np.argsort(~ok, 1, kind="stable")
    bad = rng.random((N, 8, F)) < p; np.put_along_axis(bad, where, True, 1); bad = bad & ~live[:, None]
    k = np.where(bad, R - m, m); j = np.minimum((rng.random((N, 8, F)) ** e * k).astype(np.int64), k - 1)
    return o[np.arange(8)[:, None], j + np.where(bad, m, 0)]
def pack(lo, hi, v, rest, fk, me):
    rest[:, 0] = v
    return {"at": np.ascontiguousarray(rest.reshape(N, D, 16, R).transpose(0, 2, 1, 3)).reshape(N, 16, D * R).astype(np.int32),
            "lim": np.concatenate([lo, hi], 1).reshape(N, 1, 2 * D).astype(np.int32), "fk": np.stack([gtable(x) for x in fk]), "me": me.reshape(N, 1, F).astype(np.int32)}
def whole(rng, *shape):
    return rng.integers(1 - B, B, shape)
def setup_inputs(rng):
    lo, hi, ok, v = dims(rng, rng.integers(R // 4, 3 * R // 4, 8), rng.integers(B >> 6, B >> 2, 8))
    live = living(rng.integers(C // 4, C, N), rng.random((N, F)))
    return pack(lo, hi, v, whole(rng, 8, 16, R), facts(rng, ok, live, 0.15, rng.integers(0, 8, (N, 1, F))), whole(rng, N, F))
def setup_inputs_full(rng):
    lo, hi, ok, v = dims(rng, rng.integers(R // 4, 3 * R // 4, 8), rng.integers(B >> 6, B >> 2, 8))
    n = np.full(N, C); n[rng.integers(0, N)] = 1; z = rng.random((N, F)); z[:, 0] = -1; z[:, -1] = -2
    return pack(lo, hi, v, whole(rng, 8, 16, R), facts(rng, ok, living(n, z), 0.3, rng.integers(0, 8, (N, 1, F))), whole(rng, N, F))
def setup_inputs_ends(rng):
    w = np.where(rng.permutation(8) < 3, 0, rng.integers(1, 1000, 8))
    lo, hi, ok, v = dims(rng, rng.integers(R // 4, 3 * R // 4, 8), w); h = rng.random((8, R)) < 0.5
    v = np.where(ok, np.where(h, lo, hi), np.where(h, lo - 1, hi + 1)); j = np.arange(F)
    live = living(rng.integers(C // 4, C + 1, N), np.minimum(j, F - 1 - j)[None] + np.zeros((N, 1)))
    return pack(lo, hi, v, whole(rng, 8, 16, R), facts(rng, ok, live, 0.1, rng.integers(0, 8, (N, 1, F))), whole(rng, N, F))
def setup_inputs_alike(rng):
    m = np.where(rng.permutation(8) < 4, 1, R - 1)
    lo, hi, ok, v = dims(rng, m, rng.integers(0, B >> 2, 8), np.where(rng.random(8) < 0.5, 0, R - 1))
    live = living(rng.integers(C // 4, C + 1, N), rng.random((N, F))); fk = facts(rng, ok, live, 0.1, rng.integers(0, 8, (N, 1, F)))
    q = rng.integers(0, N); s = np.flatnonzero(live[q]); fk[q][:, s] = fk[q][:, s[:1]]
    return pack(lo, hi, v, whole(rng, 8, 16, R), fk, whole(rng, N, F))
def setup_inputs_near(rng):
    lo, hi, ok, v = dims(rng, rng.integers(R // 4, 3 * R // 4, 8), rng.integers(B >> 6, B >> 2, 8))
    where = np.where(rng.random((N, 1, 1)) < 0.5, rng.integers(0, 8, (N, 1, 1)), rng.integers(0, 8, (N, 1, F)))
    live = living(rng.integers(C // 4, C + 1, N), rng.random((N, F))); sg = rng.choice(np.array([-1, 1]), (1, 16, 1))
    rest = sg * (B - 1 - rng.integers(0, 50, (8, 16, R))); me = rng.choice(np.array([-1, 1]), (N, 1)) * (B - 1 - rng.integers(0, 50, (N, F)))
    return pack(lo, hi, v, rest, facts(rng, ok, live, 0.0, where), me)
def setup_inputs_spread(rng):
    lo, hi, ok, v = dims(rng, np.maximum(1, R >> rng.integers(1, 10, 8)), 1 << rng.integers(0, 18, 8))
    live = living(np.maximum(1, C >> rng.integers(0, 6, N)), rng.random((N, F)))
    rest = whole(rng, 8, 16, R) >> rng.integers(0, 20, (8, 16, R)); me = whole(rng, N, F) >> rng.integers(0, 20, (N, F))
    return pack(lo, hi, v, rest, facts(rng, ok, live, rng.random((1, 8, 1)), rng.integers(0, 8, (N, 1, F)), 4), me)
def check_inputs(d):
    bad = [k for k in ("at", "lim", "me") if not ((d[k] > -B) & (d[k] < B)).all()]
    if not ((d["fk"] >= 0) & (d["fk"] < R)).all(): return bad + ["fk"]
    ok = passing(d["at"], d["lim"]); g = np.arange(8)[:, None]
    n = [int(np.sum(np.all(ok[g, gentries(a)], axis=0))) for a in d["fk"]]
    return bad + ([] if min(n) >= 1 and max(n) <= C else ["survivors"])
def reference(at, lim, fk, me):
    y = np.zeros((N, 16, C + 1), np.int64); ok = passing(at, lim); g = np.arange(8)[:, None]
    a = np.ascontiguousarray(at.reshape(N, 16, D, R).transpose(0, 2, 1, 3)).reshape(8, 16, R).astype(np.int64)
    for r in range(N):
        k = gentries(fk[r]); s = np.flatnonzero(np.all(ok[g, k], axis=0)); n = len(s)
        y[r, :, :n] = me[r, 0][s][None]
        for d in range(8): y[r, :, :n] += a[d][:, k[d, s]]
        y[r, :, C] = n
    return {"y": np.asarray(y, np.float32)}

@@ -1,0 +1,328 @@
+from concourse.bass import DstId, RemoteDMATransfer
+from concourse.mybir import AluOpType as A, ActivationFunctionType as AF
+import numpy as np
+
+R, F, C, D, NR = 8192, 4096, 1536, 2, 4
+TR = 3584
+EARLY = 2
+
+SCRATCH = {
+    "limi": ("sbuf", [128, 2], "int32"), "limf": ("sbuf", [128, 2], "float32"),
+    "a0": ("sbuf", [128, 128], "int32"), "cl": ("sbuf", [128, 128], "float32"),
+    "ps": ("sbuf", [128, 128], "bfloat16"),
+    "PD": ("dram", [NR, 128, 128], "bfloat16"),
+    "pw": ("sbuf", [128, R], "bfloat16"), "Pg": ("sbuf", [128, F], "bfloat16"),
+    "fkt": ("sbuf", [128, 256], "int32"), "off16": ("sbuf", [128, 256], "uint16"),
+    "fhi": ("sbuf", [128, 256], "int32"), "flo": ("sbuf", [128, 256], "int32"),
+    "fhib": ("sbuf", [128, 256], "bfloat16"), "flob": ("sbuf", [128, 256], "bfloat16"),
+    "K1": ("sbuf", [128, 512], "bfloat16"), "W1": ("sbuf", [128, TR], "bfloat16"),
+    "mei": ("sbuf", [128, 32], "int32"), "mep": ("sbuf", [128, 96], "int32"),
+    "MEL": ("sbuf", [128, 512], "bfloat16"), "MeR": ("sbuf", [128, 512], "bfloat16"),
+    "Wm": ("sbuf", [128, TR], "bfloat16"),
+    "onesb": ("sbuf", [128, 128], "bfloat16"), "onesf": ("sbuf", [128, 128], "float32"),
+    "zb": ("sbuf", [128, 128], "bfloat16"),
+    "limsel": ("sbuf", [128, 128], "float32"), "Qt": ("sbuf", [128, 260], "bfloat16"),
+    "YY": ("sbuf", [128, 144], "bfloat16"), "kc": ("sbuf", [128, 1], "int32"),
+    "kx": ("sbuf", [128, 1], "int32"), "kxf": ("sbuf", [128, 1], "float32"),
+    "ku": ("sbuf", [128, 1], "int32"), "kuf": ("sbuf", [128, 1], "float32"),
+    "row2d": ("sbuf", [128, 8], "float32"), "rowj": ("sbuf", [128, 32], "float32"),
+    "J": ("sbuf", [128, 32], "float16"),
+    "mats": ("sbuf", [128, 384], "bfloat16"), "H": ("sbuf", [128, 640], "float16"),
+    "idb": ("sbuf", [128, 128], "bfloat16"), "idf": ("sbuf", [128, 128], "float32"),
+    "sele": ("sbuf", [128, 64], "float32"),
+    "Msk": ("sbuf", [128, 32], "float16"), "Sc": ("sbuf", [128, 16], "float16"),
+    "MJ": ("sbuf", [128, 32], "float16"), "off3": ("sbuf", [128, 32], "uint16"),
+    "nt": ("sbuf", [128, 1], "float32"),
+    "Lu": ("sbuf", [128, 96], "uint16"), "Lr": ("sbuf", [128, NR * 96], "uint16"),
+    "off2": ("sbuf", [128, 96], "uint16"),
+    "ATW": ("sbuf", [128, R + 8], "int32"), "G": ("sbuf", [128, C], "float32"),
+    "SA": ("sbuf", [128, 512], "float32"), "SB": ("sbuf", [128, 256], "float32"),
+    "LA": ("sbuf", [128, 512], "float32"), "LB": ("sbuf", [128, 256], "float32"),
+    "accA": ("sbuf", [128, 128], "float32"), "accB": ("sbuf", [128, 64], "float32"),
+    "OA": ("sbuf", [128, 128], "float32"), "OB": ("sbuf", [128, 128], "float32"),
+}
+for _b in range(8):
+    SCRATCH["b%d" % _b] = ("psum", [128, 512], "float32")
+NEV = 125
+SEMAPHORES = (["e%d" % _i for _i in range(NEV)] + ["left", "h1"] + ["h2_%d" % _q for _q in range(NR)]
+              + ["h3a_%d" % _q for _q in range(NR)] + ["h3b_%d" % _q for _q in range(NR)])
+
+
+def rank_program(g, core, T, topo):
+    q = T.rank_of(core)
+    if q is None:
+        return
+    V, S, PE, SY = g.vector, g.scalar, g.tensor, g.sync
+    queues = {"g": g, "v": V, "s": S, "p": PE, "y": SY}
+    used, total, seen, waited = [0], {}, {}, {}
+
+    def ev(inst, n=1, s=None):
+        if s is None:
+            s = new()
+        inst.then_inc(T.sem[s], n)
+        total[s] = total.get(s, 0) + n
+        return s
+
+    def new():
+        s = "e%d" % used[0]
+        used[0] += 1
+        return s
+
+    def wait(k, *names):
+        for s in names:
+            n = total[s]
+            if seen.get((k, s), 0) < n:
+                queues[k].wait_ge(T.sem[s], n)
+                seen[(k, s)] = n
+                waited[s] = max(waited.get(s, 0), n)
+
+    others = [c for c in T.cores if c != core]
+    cross = [c for c in others if topo.die(c) != topo.die(core)]
+    same = [c for c in others if topo.die(c) == topo.die(core)]
+    dests = cross[:1] + same + cross[1:]
+
+    def send(rsem, src, dst):
+        tr = []
+        for k, c in enumerate(dests):
+            rid, pid, _ = topo.addr(c)
+            mask = sum(1 << e for e in topo.engines(core, c)[k::4])
+            tr.append(RemoteDMATransfer(dst_ids=[DstId(rid=rid, pnc=pid)], dma_engine_mask=mask,
+                                        remote_sem=T.sem[rsem], src=src(T.rank_of(c)), dst=dst))
+        g.remote_dma_fused(tr, local_sem=T.sem.left)
+        total["left"] = total.get("left", 0) + 4 * len(dests)
+
+    def at_load(k):
+        r, e = k // 2, k % 2
+        p = 32 * r + 16 * e
+        return SY.dma_start(T.ATW[p:p + 16, 0:R], T.at[:, R * e:R * e + R])
+
+    d_lim = ev(SY.dma_start(T.limi[0:2, :], T.lim[0:1, :]), 16)
+    d_a0 = ev(SY.dma_start(T.a0[:, :], T.at[0:1, :]), 16)
+    d_fk = ev(S.dma_start(T.fkt[:, :], T.fk[:, :]), 16)
+    d_me = ev(S.dma_start(T.mei[:, 0:16], T.me[0:1, 0:2048]), 16)
+    ev(S.dma_start(T.mei[:, 16:32], T.me[0:1, 2048:4096]), 16, d_me)
+    d_at = new()
+    for k in range(EARLY):
+        ev(at_load(k), 16, d_at)
+
+    m_one = ev(V.memset(T.onesf[:, :], 1.0))
+    ev(V.memset(T.onesb[:, :], 1.0), 1, m_one)
+    m_z = ev(V.memset(T.zb[:, :], 0.0))
+    ev(V.memset(T.Qt[:, :], 0.0), 1, m_z)
+    z0 = ev(V.memset(T.pw[:, 0:2048], 0.0))
+    z1 = ev(V.memset(T.pw[:, 2048:4096], 0.0))
+    wait("s", z0)
+    z2 = ev(S.activation(T.pw[:, 4096:6144], T.pw[:, 0:2048], AF.Copy))
+    ev(S.activation(T.pw[:, 6144:8192], T.pw[:, 0:2048], AF.Copy), 1, z2)
+
+    wait("g", m_one)
+    c_lim = ev(g.affine_select(T.limsel[0:2, :], T.onesf[0:2, :], [[1, 2], [0, 64]], A.is_equal, 0.0, 0, -1))
+    wait("g", m_z)
+    c_q = new()
+    for h in range(2):
+        ev(g.affine_select(T.Qt[:, 130 * h + 1:130 * h + 129:2], T.onesb[:, 0:64], [[2, 8], [16, 8]],
+                           A.is_equal, 0.0, h, -1), 1, c_q)
+    c_io = ev(g.iota(T.kc[:, :], [[0, 1]], 0, 1))
+    ev(g.iota(T.row2d[:, :], [[2, 8]], 0, 0, allow_small_or_imprecise_dtypes=True), 1, c_io)
+    ev(g.iota(T.rowj[:, :], [[1, 2], [32, 16]], C, 0, allow_small_or_imprecise_dtypes=True), 1, c_io)
+
+    wait("v", d_lim)
+    v_lim = ev(V.tensor_copy(T.limf[0:2, :], T.limi[0:2, :]))
+    wait("p", v_lim, c_lim)
+    p_lim = ev(PE.matmul(T.b2[:, 480:482], T.limsel[0:2, :], T.limf[0:2, :], True, True))
+    wait("v", d_a0, p_lim)
+    v_cl = ev(V.tensor_scalar(out=T.cl[:, :], in0=T.a0[:, :], scalar1=T.b2[:, 480:481], scalar2=T.b2[:, 481:482],
+                              op0=A.max, op1=A.min))
+    wait("v", v_cl)
+    v_ps = ev(V.tensor_tensor(T.ps[:, :], T.cl[:, :], T.a0[:, :], A.is_equal))
+    wait("g", v_ps)
+    send("h1", lambda r: T.ps[:, :], T.PD[q])
+    wait("y", v_ps)
+    d_own = ev(SY.dma_start(T.PD[q], T.ps[:, :]), 16)
+    total["h1"] = 12
+    wait("y", d_own, z1, z2, "h1")
+    d_pw = ev(SY.dma_start(T.pw[0:128:16, :], T.PD[:, :, :]), 16)
+    wait("y", d_pw)
+    for k in range(EARLY, 8):
+        ev(at_load(k), 16, d_at)
+
+    wait("v", d_fk)
+    v_off = ev(V.tensor_copy(T.off16[:, :], T.fkt[:, :]))
+    v_k = ev(V.tensor_scalar(out=T.fhi[:, :], in0=T.fkt[:, :], scalar1=0x1F80, scalar2=None, op0=A.bitwise_and))
+    ev(V.tensor_scalar(out=T.flo[:, :], in0=T.fkt[:, :], scalar1=127, scalar2=None, op0=A.bitwise_and), 1, v_k)
+    wait("v", v_k)
+    v_kb = ev(V.tensor_scalar(out=T.fhib[:, :], in0=T.fhi[:, :], scalar1=-8192.0, scalar2=None, op0=A.add))
+    ev(V.tensor_copy(T.flob[:, :], T.flo[:, :]), 1, v_kb)
+    wait("p", v_kb, c_q)
+    p_r = new()
+    for h in range(2):
+        o = T.b0[:, 256 * h:256 * h + 256]
+        ev(PE.matmul(o, T.Qt[:, 130 * h + 1:130 * h + 129], T.fhib[:, :], True, False), 1, p_r)
+        ev(PE.matmul(o, T.Qt[:, 130 * h:130 * h + 128], T.flob[:, :], False, True), 1, p_r)
+    wait("s", p_r)
+    s_k1 = ev(S.activation(T.K1[:, :], T.b0[:, :], AF.Copy))
+
+    c_m = new()
+    pat = [[1, 8], [8, 16]]
+    ev(g.affine_select(T.mats[:, 0:128], T.zb[:, :], pat, A.is_gt, -1.0, 0, -1), 1, c_m)
+    ev(g.affine_select(T.mats[:, 128:256], T.zb[:, :], pat, A.is_ge, -1.0, 0, -1), 1, c_m)
+    ev(g.affine_select(T.mats[:, 256:384], T.onesb[:, :], pat, A.is_equal, 0.0, 0, -1), 1, c_m)
+    c_idb = ev(g.affine_select(T.idb[:, :], T.onesb[:, :], [[1, 128]], A.is_equal, 0.0, 0, -1))
+    c_s1 = ev(g.affine_select(T.sele[:, :], T.onesf[:, 0:64], [[32, 4], [1, 16]], A.is_equal, 0.0, 0, -1))
+    c_idf = ev(g.affine_select(T.idf[:, :], T.onesf[:, :], [[1, 128]], A.is_equal, 0.0, 0, -1))
+    wait("g", c_s1)
+    c_sel = ev(g.affine_select(T.sele[:, :], T.sele[:, :], [[32, 4], [1, 16]], A.not_equal, 1.0, 16, -1))
+
+    m_mel = ev(V.memset(T.MEL[:, :], 0.0))
+    wait("v", d_me, c_io)
+    v_mp = ev(V.tensor_scalar(out=T.mep[:, 0:32], in0=T.mei[:, :], scalar1=14, scalar2=None, op0=A.arith_shift_right))
+    ev(V.tensor_scalar(out=T.mep[:, 32:64], in0=T.mei[:, :], scalar1=0x3F80, scalar2=None, op0=A.bitwise_and), 1, v_mp)
+    ev(V.tensor_scalar(out=T.mep[:, 64:96], in0=T.mei[:, :], scalar1=127, scalar2=None, op0=A.bitwise_and), 1, v_mp)
+    v_kx = ev(V.tensor_scalar(out=T.kx[:, :], in0=T.kc[:, :], scalar1=14, scalar2=None, op0=A.bitwise_and))
+    ev(V.tensor_scalar(out=T.ku[:, :], in0=T.kc[:, :], scalar1=3, scalar2=None, op0=A.arith_shift_right), 1, v_kx)
+    m_yy = ev(V.memset(T.YY[:, :], 0.0))
+    ev(V.memset(T.W1[:, 0:C], 0.0), 1, m_yy)
+    wait("v", v_mp, m_mel)
+    v_mel = new()
+    for x in range(3):
+        for h in range(2):
+            ev(V.tensor_scalar(out=T.MEL[:, 256 * h + x:256 * h + 256:16], in0=T.mep[:, 32 * x + h:32 * x + 32:2],
+                               scalar1=16384.0 if x == 0 else 1.0, scalar2=None, op0=A.mult), 1, v_mel)
+    wait("v", v_kx, m_yy)
+    v_kf = ev(V.tensor_copy(T.kxf[:, :], T.kx[:, :]))
+    ev(V.tensor_scalar(out=T.kuf[:, :], in0=T.ku[:, :], scalar1=2.0, scalar2=None, op0=A.mult), 1, v_kf)
+    wait("v", c_m)
+    v_h = ev(V.tensor_copy(T.H[:, 0:384], T.mats[:, :]))
+    ev(V.tensor_scalar(out=T.H[:, 384:512], in0=T.mats[:, 256:384], scalar1=-1.0, scalar2=None, op0=A.mult), 1, v_h)
+    ev(V.tensor_copy(T.H[:, 512:640], T.onesb[:, :]), 1, v_h)
+    wait("v", v_kf)
+    v_yy = ev(V.tensor_scalar(out=T.YY[:, 15:143:16], in0=T.row2d[:, :], scalar1=T.kxf[:, :], scalar2=None,
+                              op0=A.is_equal))
+    v_j = ev(V.tensor_scalar(out=T.J[:, :], in0=T.rowj[:, :], scalar1=T.kuf[:, :], scalar2=None, op0=A.add))
+    L1, L1B, IP, NIP, ONE = [T.H[:, 128 * k:128 * k + 128] for k in range(5)]
+    wait("p", v_mel, c_idb)
+    p_me = new()
+    for x in range(4):
+        ev(PE.matmul(T.b1[:, 128 * x:128 * x + 128], T.MEL[:, 128 * x:128 * x + 128], T.idb[:, :], True, True), 1, p_me)
+    wait("p", v_h, v_j)
+    PE.matmul(T.b3[:, 0:32], IP, T.J[:, :], True, False)
+    wait("s", p_me)
+    s_mer = ev(S.activation(T.MeR[:, :], T.b1[:, :], AF.Copy))
+
+    wait("v", d_pw, v_off, z1)
+    wait("s", d_pw, v_off)
+    got = {}
+    for c in range(2):
+        j, u = 1024 * c, 64 * c
+        got[c] = ev(V.tensor_copy(T.Pg[:, j:j + 1024], T.pw[:, :].indirect(T.off16[:, u:u + 64])))
+        j, u = j + 2048, u + 128
+        got[2 + c] = ev(S.activation(T.Pg[:, j:j + 1024], T.pw[:, :].indirect(T.off16[:, u:u + 64]), AF.Copy))
+    p_c = new()
+    for c in (0, 2, 1, 3):
+        wait("p", got[c])
+        for uh in range(4 * c, 4 * c + 4):
+            for h in range(2):
+                w = 16 * h + uh
+                ev(PE.matmul(T.b2[:, w:w + 1], T.Pg[:, 256 * uh + h:256 * uh + 256:2], T.onesb[:, 0:1], True, True), 1, p_c)
+    wait("v", p_c)
+    v_m = ev(V.tensor_scalar(out=T.Msk[:, :], in0=T.b2[:, 0:32], scalar1=7.5, scalar2=None, op0=A.is_gt))
+    wait("v", v_m)
+    v_sc = ev(V.tensor_tensor_scan(T.Sc[:, :], T.Msk[:, 0:16], T.Msk[:, 16:32], 0.0, A.add, A.add))
+    v_mj = ev(V.tensor_tensor(T.MJ[:, :], T.Msk[:, :], T.J[:, :], A.mult))
+    wait("p", v_m)
+    PE.matmul(T.b3[:, 0:32], L1, T.Msk[:, :], False, False)
+    PE.matmul(T.b3[:, 0:16], L1, T.Msk[:, 16:32], False, False)
+    PE.matmul(T.b3[:, 16:32], L1B, T.Msk[:, 0:16], False, False)
+    wait("p", v_sc)
+    PE.matmul(T.b3[:, 0:16], ONE, T.Sc[:, :], False, False)
+    PE.matmul(T.b3[:, 16:32], ONE, T.Sc[:, :], False, False)
+    wait("p", v_mj)
+    p_pos = ev(PE.matmul(T.b3[:, 0:32], NIP, T.MJ[:, :], False, True))
+    p_nt = ev(PE.matmul(T.b7[:, 256:257], ONE, T.Sc[:, 15:16], True, True))
+    wait("v", p_pos)
+    v_o3 = ev(V.tensor_copy(T.off3[:, :], T.b3[:, 0:32]))
+    wait("s", p_nt)
+    s_nt = ev(S.activation(T.nt[:, :], T.b7[:, 256:257], AF.Copy))
+
+    wait("v", v_o3, s_k1)
+    v_w1 = ev(V.tensor_copy(T.W1[:, :].indirect(T.off3[:, :]), T.K1[:, :]))
+    m_w = ev(V.memset(T.Wm[:, 0:C], 0.0))
+    ev(V.memset(T.ATW[:, R:R + 8], 0), 1, m_w)
+    wait("p", v_w1, v_yy)
+    for i in range(16):
+        last = PE.matmul(T.b4[:, 0:96], T.YY[:, 15 - i:143 - i], T.W1[:, i:C:16], i == 0, i == 15)
+    p_l = ev(last)
+    wait("v", p_l)
+    v_lu = ev(V.tensor_scalar(out=T.Lu[:, :], in0=T.b4[:, 0:96], scalar1=8192.0, scalar2=None, op0=A.add))
+    wait("g", v_lu)
+    send("h2_%d" % q, lambda r: T.Lu[:, :], T.Lr[:, 96 * q:96 * q + 96])
+    wait("g", s_nt)
+    ev(g.dma_start(T.y[:, C:C + 1], T.nt[0:16, :], allow_slow_non_contiguous=True), 16)
+
+    wait("v", s_mer, m_w)
+    v_wm = ev(V.tensor_copy(T.Wm[:, :].indirect(T.off3[:, :]), T.MeR[:, :]))
+    wait("p", v_wm, s_nt)
+    p_m = new()
+    for c in range(12):
+        o = T.b7[:, c:128:8] if c < 8 else T.b7[:, 128 + c - 8:192:4]
+        ev(PE.matmul(o, T.Wm[:, 128 * c:128 * c + 128], T.onesb[:, 0:16], True, True), 1, p_m)
+
+    v_o2 = new()
+    order = [q] + [T.rank_of(c) for c in dests]
+    for r in order:
+        if r == q:
+            wait("v", v_lu)
+            src = T.Lu[32 * q:32 * q + 32, :]
+        else:
+            total["h2_%d" % r] = 4
+            wait("v", "h2_%d" % r)
+            src = T.Lr[32 * q:32 * q + 32, 96 * r:96 * r + 96]
+        ev(V.tensor_copy(T.off2[32 * r:32 * r + 32, :], src), 1, v_o2)
+    wait("v", v_o2, d_at)
+    pc = {}
+    wait("p", c_sel)
+    for c in range(12):
+        e = ev(V.tensor_copy(T.G[:, 128 * c:128 * c + 128], T.ATW[:, :].indirect(T.off2[:, 8 * c:8 * c + 8])))
+        wait("p", e)
+        o = T.b5[:, c:512:8] if c < 8 else T.b6[:, c - 8:256:4]
+        m = PE.matmul(o, T.G[:, 128 * c:128 * c + 128], T.sele[:, :], True, True)
+        if c in (0, 8):
+            pc[c // 8] = new()
+        ev(m, 1, pc[c // 8])
+        if c == 7:
+            wait("s", pc[0])
+            s_sa = ev(S.activation(T.SA[:, :], T.b5[:, :], AF.Copy))
+            wait("g", s_sa)
+            send("h3a_%d" % q, lambda r: T.SA[:, 128 * r:128 * r + 128], T.LA[:, 128 * q:128 * q + 128])
+    wait("v", pc[1])
+    v_sb = ev(V.tensor_copy(T.SB[:, :], T.b6[:, 0:256]))
+    wait("g", v_sb)
+    send("h3b_%d" % q, lambda r: T.SB[:, 64 * r:64 * r + 64], T.LB[:, 64 * q:64 * q + 64])
+
+    wait("v", s_sa, v_sb, p_m)
+    a = ev(V.tensor_tensor(T.accA[:, :], T.SA[:, 128 * q:128 * q + 128], T.b7[:, 0:128], A.add))
+    b = ev(V.tensor_tensor(T.accB[:, :], T.SB[:, 64 * q:64 * q + 64], T.b7[:, 128:192], A.add))
+    for r in order[1:]:
+        total["h3a_%d" % r] = 4
+        wait("v", "h3a_%d" % r, a)
+        a = ev(V.tensor_tensor(T.accA[:, :], T.accA[:, :], T.LA[:, 128 * r:128 * r + 128], A.add))
+    wait("p", a, c_idf)
+    p_a = ev(PE.matmul(T.b0[:, 0:128], T.accA[:, :], T.idf[:, :], True, True))
+    wait("s", p_a)
+    s_oa = ev(S.activation(T.OA[:, :], T.b0[:, 0:128], AF.Copy))
+    wait("y", s_oa)
+    ev(SY.dma_start(T.y[:, 0:1024], T.OA[:, :]), 16)
+    for r in order[1:]:
+        total["h3b_%d" % r] = 4
+        wait("v", "h3b_%d" % r, b)
+        b = ev(V.tensor_tensor(T.accB[:, :], T.accB[:, :], T.LB[:, 64 * r:64 * r + 64], A.add))
+    wait("p", b)
+    p_b = ev(PE.matmul(T.b1[0:64, 0:128], T.accB[:, :], T.idf[:, :], True, True))
+    wait("v", p_b)
+    v_ob = ev(V.tensor_copy(T.OB[0:64, :], T.b1[0:64, 0:128]))
+    wait("s", v_ob)
+    ev(S.dma_start(T.y[:, 1024:1536], T.OB[0:64, :]), 16)
+
+    for s in total:
+        if waited.get(s, 0) < total[s]:
+            wait("g", s)

@@ -5,11 +5,11 @@ import numpy as np
 R, F, C, D, NR = 8192, 4096, 1536, 2, 4
 TR = 3584
 EARLY = 2
+P1, P2 = 2560, 4608
 
 SCRATCH = {
     "limi": ("sbuf", [128, 2], "int32"), "limf": ("sbuf", [128, 2], "float32"),
-    "a0": ("sbuf", [128, 128], "int32"), "cl": ("sbuf", [128, 128], "float32"),
-    "ps": ("sbuf", [128, 128], "bfloat16"),
+    "a0": ("sbuf", [128, 128], "int32"), "ps": ("sbuf", [128, 128], "bfloat16"),
     "PD": ("dram", [NR, 128, 128], "bfloat16"),
     "pw": ("sbuf", [128, R], "bfloat16"), "Pg": ("sbuf", [128, F], "bfloat16"),
     "fkt": ("sbuf", [128, 256], "int32"), "off16": ("sbuf", [128, 256], "uint16"),
@@ -36,16 +36,17 @@ SCRATCH = {
     "Lu": ("sbuf", [128, 96], "uint16"), "Lr": ("sbuf", [128, NR * 96], "uint16"),
     "off2": ("sbuf", [128, 96], "uint16"),
     "ATW": ("sbuf", [128, R + 8], "int32"), "G": ("sbuf", [128, C], "float32"),
-    "SA": ("sbuf", [128, 512], "float32"), "SB": ("sbuf", [128, 256], "float32"),
-    "LA": ("sbuf", [128, 512], "float32"), "LB": ("sbuf", [128, 256], "float32"),
-    "accA": ("sbuf", [128, 128], "float32"), "accB": ("sbuf", [128, 64], "float32"),
-    "OA": ("sbuf", [128, 128], "float32"), "OB": ("sbuf", [128, 128], "float32"),
+    "SA": ("sbuf", [128, 512], "float32"), "LA": ("sbuf", [128, 512], "float32"),
+    "SB0": ("sbuf", [128, 128], "float32"), "LB0": ("sbuf", [128, 128], "float32"),
+    "SB1": ("sbuf", [128, 128], "float32"), "LB1": ("sbuf", [128, 128], "float32"),
+    "accA": ("sbuf", [128, 128], "float32"), "tB": ("sbuf", [128, 64], "float32"),
+    "OA": ("sbuf", [128, 128], "float32"), "OB": ("sbuf", [128, 64], "float32"),
 }
 for _b in range(8):
     SCRATCH["b%d" % _b] = ("psum", [128, 512], "float32")
-NEV = 125
-SEMAPHORES = (["e%d" % _i for _i in range(NEV)] + ["left", "h1"] + ["h2_%d" % _q for _q in range(NR)]
-              + ["h3a_%d" % _q for _q in range(NR)] + ["h3b_%d" % _q for _q in range(NR)])
+NEV = 122
+SEMAPHORES = (["e%d" % _i for _i in range(NEV)] + ["left", "h1"]
+              + ["%s_%d" % (_n, _q) for _n in ("h2", "h3a", "h3b0", "h3b1") for _q in range(NR)])
 
 
 def rank_program(g, core, T, topo):
@@ -56,16 +57,16 @@ def rank_program(g, core, T, topo):
     queues = {"g": g, "v": V, "s": S, "p": PE, "y": SY}
     used, total, seen, waited = [0], {}, {}, {}
 
+    def new():
+        s = "e%d" % used[0]
+        used[0] += 1
+        return s
+
     def ev(inst, n=1, s=None):
         if s is None:
             s = new()
         inst.then_inc(T.sem[s], n)
         total[s] = total.get(s, 0) + n
-        return s
-
-    def new():
-        s = "e%d" % used[0]
-        used[0] += 1
         return s
 
     def wait(k, *names):
@@ -80,6 +81,11 @@ def rank_program(g, core, T, topo):
     cross = [c for c in others if topo.die(c) != topo.die(core)]
     same = [c for c in others if topo.die(c) == topo.die(core)]
     dests = cross[:1] + same + cross[1:]
+    order = [T.rank_of(c) for c in dests]
+    total["h1"] = 12
+    for n in ("h2", "h3a", "h3b0", "h3b1"):
+        for r in order:
+            total["%s_%d" % (n, r)] = 4
 
     def send(rsem, src, dst):
         tr = []
@@ -97,23 +103,25 @@ def rank_program(g, core, T, topo):
         return SY.dma_start(T.ATW[p:p + 16, 0:R], T.at[:, R * e:R * e + R])
 
     d_lim = ev(SY.dma_start(T.limi[0:2, :], T.lim[0:1, :]), 16)
-    d_a0 = ev(SY.dma_start(T.a0[:, :], T.at[0:1, :]), 16)
+    d_a0 = ev(S.dma_start(T.a0[:, :], T.at[0:1, :]), 16)
     d_fk = ev(S.dma_start(T.fkt[:, :], T.fk[:, :]), 16)
-    d_me = ev(S.dma_start(T.mei[:, 0:16], T.me[0:1, 0:2048]), 16)
-    ev(S.dma_start(T.mei[:, 16:32], T.me[0:1, 2048:4096]), 16, d_me)
+    d_me = ev(SY.dma_start(T.mei[:, 0:16], T.me[0:1, 0:2048]), 16)
+    ev(SY.dma_start(T.mei[:, 16:32], T.me[0:1, 2048:4096]), 16, d_me)
     d_at = new()
     for k in range(EARLY):
         ev(at_load(k), 16, d_at)
 
+    z0 = ev(V.memset(T.pw[:, 0:1024], 0.0))
     m_one = ev(V.memset(T.onesf[:, :], 1.0))
     ev(V.memset(T.onesb[:, :], 1.0), 1, m_one)
     m_z = ev(V.memset(T.zb[:, :], 0.0))
     ev(V.memset(T.Qt[:, :], 0.0), 1, m_z)
-    z0 = ev(V.memset(T.pw[:, 0:2048], 0.0))
-    z1 = ev(V.memset(T.pw[:, 2048:4096], 0.0))
+    z1 = ev(V.memset(T.pw[:, 1024:P1], 0.0))
     wait("s", z0)
-    z2 = ev(S.activation(T.pw[:, 4096:6144], T.pw[:, 0:2048], AF.Copy))
-    ev(S.activation(T.pw[:, 6144:8192], T.pw[:, 0:2048], AF.Copy), 1, z2)
+    z2 = new()
+    for k in range(P2, R, 1024):
+        n = min(1024, R - k)
+        ev(S.activation(T.pw[:, k:k + n], T.pw[:, 0:n], AF.Copy), 1, z2)
 
     wait("g", m_one)
     c_lim = ev(g.affine_select(T.limsel[0:2, :], T.onesf[0:2, :], [[1, 2], [0, 64]], A.is_equal, 0.0, 0, -1))
@@ -131,18 +139,19 @@ def rank_program(g, core, T, topo):
     wait("p", v_lim, c_lim)
     p_lim = ev(PE.matmul(T.b2[:, 480:482], T.limsel[0:2, :], T.limf[0:2, :], True, True))
     wait("v", d_a0, p_lim)
-    v_cl = ev(V.tensor_scalar(out=T.cl[:, :], in0=T.a0[:, :], scalar1=T.b2[:, 480:481], scalar2=T.b2[:, 481:482],
-                              op0=A.max, op1=A.min))
+    v_cl = ev(V.tensor_scalar(out=T.b2[:, 128:256], in0=T.a0[:, :], scalar1=T.b2[:, 480:481],
+                              scalar2=T.b2[:, 481:482], op0=A.max, op1=A.min))
     wait("v", v_cl)
-    v_ps = ev(V.tensor_tensor(T.ps[:, :], T.cl[:, :], T.a0[:, :], A.is_equal))
+    v_ps = ev(V.tensor_tensor(T.ps[:, :], T.b2[:, 128:256], T.a0[:, :], A.is_equal))
     wait("g", v_ps)
     send("h1", lambda r: T.ps[:, :], T.PD[q])
-    wait("y", v_ps)
-    d_own = ev(SY.dma_start(T.PD[q], T.ps[:, :]), 16)
-    total["h1"] = 12
-    wait("y", d_own, z1, z2, "h1")
-    d_pw = ev(SY.dma_start(T.pw[0:128:16, :], T.PD[:, :, :]), 16)
-    wait("y", d_pw)
+    ev(V.memset(T.pw[:, P1:P2], 0.0), 1, z1)
+    wait("y", v_ps, z0, z1, z2)
+    d_pw = ev(SY.dma_start(T.pw[32 * q:32 * q + 32:16, :], T.ps[:, :]), 16)
+    wait("y", "h1")
+    for lo, hi in ((0, q), (q + 1, NR)):
+        if lo < hi:
+            ev(SY.dma_start(T.pw[32 * lo:32 * hi:16, :], T.PD[lo:hi]), 16, d_pw)
     for k in range(EARLY, 8):
         ev(at_load(k), 16, d_at)
 
@@ -162,68 +171,68 @@ def rank_program(g, core, T, topo):
     wait("s", p_r)
     s_k1 = ev(S.activation(T.K1[:, :], T.b0[:, :], AF.Copy))
 
+    c_idb = ev(g.affine_select(T.idb[:, :], T.onesb[:, :], [[1, 128]], A.is_equal, 0.0, 0, -1))
     c_m = new()
     pat = [[1, 8], [8, 16]]
     ev(g.affine_select(T.mats[:, 0:128], T.zb[:, :], pat, A.is_gt, -1.0, 0, -1), 1, c_m)
     ev(g.affine_select(T.mats[:, 128:256], T.zb[:, :], pat, A.is_ge, -1.0, 0, -1), 1, c_m)
     ev(g.affine_select(T.mats[:, 256:384], T.onesb[:, :], pat, A.is_equal, 0.0, 0, -1), 1, c_m)
-    c_idb = ev(g.affine_select(T.idb[:, :], T.onesb[:, :], [[1, 128]], A.is_equal, 0.0, 0, -1))
+    z_w1 = ev(g.iota(T.W1[:, 0:C], [[0, C]], 0, 0, allow_small_or_imprecise_dtypes=True))
     c_s1 = ev(g.affine_select(T.sele[:, :], T.onesf[:, 0:64], [[32, 4], [1, 16]], A.is_equal, 0.0, 0, -1))
     c_idf = ev(g.affine_select(T.idf[:, :], T.onesf[:, :], [[1, 128]], A.is_equal, 0.0, 0, -1))
     wait("g", c_s1)
     c_sel = ev(g.affine_select(T.sele[:, :], T.sele[:, :], [[32, 4], [1, 16]], A.not_equal, 1.0, 16, -1))
 
+    m_w = ev(V.memset(T.ATW[:, R:R + 8], 0))
     m_mel = ev(V.memset(T.MEL[:, :], 0.0))
     wait("v", d_me, c_io)
     v_mp = ev(V.tensor_scalar(out=T.mep[:, 0:32], in0=T.mei[:, :], scalar1=14, scalar2=None, op0=A.arith_shift_right))
     ev(V.tensor_scalar(out=T.mep[:, 32:64], in0=T.mei[:, :], scalar1=0x3F80, scalar2=None, op0=A.bitwise_and), 1, v_mp)
     ev(V.tensor_scalar(out=T.mep[:, 64:96], in0=T.mei[:, :], scalar1=127, scalar2=None, op0=A.bitwise_and), 1, v_mp)
+    v_ku = ev(V.tensor_scalar(out=T.ku[:, :], in0=T.kc[:, :], scalar1=3, scalar2=None, op0=A.arith_shift_right))
     v_kx = ev(V.tensor_scalar(out=T.kx[:, :], in0=T.kc[:, :], scalar1=14, scalar2=None, op0=A.bitwise_and))
-    ev(V.tensor_scalar(out=T.ku[:, :], in0=T.kc[:, :], scalar1=3, scalar2=None, op0=A.arith_shift_right), 1, v_kx)
-    m_yy = ev(V.memset(T.YY[:, :], 0.0))
-    ev(V.memset(T.W1[:, 0:C], 0.0), 1, m_yy)
     wait("v", v_mp, m_mel)
     v_mel = new()
     for x in range(3):
         for h in range(2):
             ev(V.tensor_scalar(out=T.MEL[:, 256 * h + x:256 * h + 256:16], in0=T.mep[:, 32 * x + h:32 * x + 32:2],
                                scalar1=16384.0 if x == 0 else 1.0, scalar2=None, op0=A.mult), 1, v_mel)
-    wait("v", v_kx, m_yy)
-    v_kf = ev(V.tensor_copy(T.kxf[:, :], T.kx[:, :]))
-    ev(V.tensor_scalar(out=T.kuf[:, :], in0=T.ku[:, :], scalar1=2.0, scalar2=None, op0=A.mult), 1, v_kf)
-    wait("v", c_m)
-    v_h = ev(V.tensor_copy(T.H[:, 0:384], T.mats[:, :]))
-    ev(V.tensor_scalar(out=T.H[:, 384:512], in0=T.mats[:, 256:384], scalar1=-1.0, scalar2=None, op0=A.mult), 1, v_h)
-    ev(V.tensor_copy(T.H[:, 512:640], T.onesb[:, :]), 1, v_h)
-    wait("v", v_kf)
-    v_yy = ev(V.tensor_scalar(out=T.YY[:, 15:143:16], in0=T.row2d[:, :], scalar1=T.kxf[:, :], scalar2=None,
-                              op0=A.is_equal))
-    v_j = ev(V.tensor_scalar(out=T.J[:, :], in0=T.rowj[:, :], scalar1=T.kuf[:, :], scalar2=None, op0=A.add))
-    L1, L1B, IP, NIP, ONE = [T.H[:, 128 * k:128 * k + 128] for k in range(5)]
+    wait("v", v_ku)
+    v_kf = ev(V.tensor_scalar(out=T.kuf[:, :], in0=T.ku[:, :], scalar1=2.0, scalar2=None, op0=A.mult))
     wait("p", v_mel, c_idb)
     p_me = new()
     for x in range(4):
         ev(PE.matmul(T.b1[:, 128 * x:128 * x + 128], T.MEL[:, 128 * x:128 * x + 128], T.idb[:, :], True, True), 1, p_me)
-    wait("p", v_h, v_j)
-    PE.matmul(T.b3[:, 0:32], IP, T.J[:, :], True, False)
+
+    wait("v", d_pw, v_off, z0, z1)
+    wait("s", d_pw, v_off, z0, z1)
+    p_c = new()
+    vgot = []
+    for lo, hi in ((0, 3), (3, 5), (5, 7), (7, 8)):
+        got = [ev(V.tensor_copy(T.Pg[:, 256 * lo:256 * hi], T.pw[:, :].indirect(T.off16[:, 16 * lo:16 * hi]))),
+               ev(S.activation(T.Pg[:, 2048 + 256 * lo:2048 + 256 * hi],
+                               T.pw[:, :].indirect(T.off16[:, 128 + 16 * lo:128 + 16 * hi]), AF.Copy))]
+        vgot.append(got[0])
+        for b in range(2):
+            wait("p", got[b])
+            for uh in range(8 * b + lo, 8 * b + hi):
+                for h in range(2):
+                    w = 16 * h + uh
+                    ev(PE.matmul(T.b2[:, w:w + 1], T.Pg[:, 256 * uh + h:256 * uh + 256:2], T.onesb[:, 0:1], True, True),
+                       1, p_c)
     wait("s", p_me)
     s_mer = ev(S.activation(T.MeR[:, :], T.b1[:, :], AF.Copy))
+    wait("s", *vgot)
+    z_wm = ev(S.activation(T.Wm[:, 0:C], T.Pg[:, 0:C], AF.Copy, scale=0.0))
 
-    wait("v", d_pw, v_off, z1)
-    wait("s", d_pw, v_off)
-    got = {}
-    for c in range(2):
-        j, u = 1024 * c, 64 * c
-        got[c] = ev(V.tensor_copy(T.Pg[:, j:j + 1024], T.pw[:, :].indirect(T.off16[:, u:u + 64])))
-        j, u = j + 2048, u + 128
-        got[2 + c] = ev(S.activation(T.Pg[:, j:j + 1024], T.pw[:, :].indirect(T.off16[:, u:u + 64]), AF.Copy))
-    p_c = new()
-    for c in (0, 2, 1, 3):
-        wait("p", got[c])
-        for uh in range(4 * c, 4 * c + 4):
-            for h in range(2):
-                w = 16 * h + uh
-                ev(PE.matmul(T.b2[:, w:w + 1], T.Pg[:, 256 * uh + h:256 * uh + 256:2], T.onesb[:, 0:1], True, True), 1, p_c)
+    wait("v", c_m, v_kf)
+    v_h = ev(V.tensor_copy(T.H[:, 0:384], T.mats[:, :]))
+    v_j = ev(V.tensor_scalar(out=T.J[:, :], in0=T.rowj[:, :], scalar1=T.kuf[:, :], scalar2=None, op0=A.add))
+    ev(V.tensor_copy(T.H[:, 512:640], T.onesb[:, :]), 1, v_h)
+    ev(V.tensor_scalar(out=T.H[:, 384:512], in0=T.mats[:, 256:384], scalar1=-1.0, scalar2=None, op0=A.mult), 1, v_h)
+    L1, L1B, IP, NIP, ONE = [T.H[:, 128 * k:128 * k + 128] for k in range(5)]
+    wait("p", v_h, v_j)
+    PE.matmul(T.b3[:, 0:32], IP, T.J[:, :], True, False)
     wait("v", p_c)
     v_m = ev(V.tensor_scalar(out=T.Msk[:, :], in0=T.b2[:, 0:32], scalar1=7.5, scalar2=None, op0=A.is_gt))
     wait("v", v_m)
@@ -239,15 +248,21 @@ def rank_program(g, core, T, topo):
     wait("p", v_mj)
     p_pos = ev(PE.matmul(T.b3[:, 0:32], NIP, T.MJ[:, :], False, True))
     p_nt = ev(PE.matmul(T.b7[:, 256:257], ONE, T.Sc[:, 15:16], True, True))
+    wait("v", v_kx)
+    v_kf2 = ev(V.tensor_copy(T.kxf[:, :], T.kx[:, :]))
+    m_yy = ev(V.memset(T.YY[:, :], 0.0))
+    wait("v", v_kf2, m_yy)
+    v_yy = ev(V.tensor_scalar(out=T.YY[:, 15:143:16], in0=T.row2d[:, :], scalar1=T.kxf[:, :], scalar2=None,
+                              op0=A.is_equal))
     wait("v", p_pos)
     v_o3 = ev(V.tensor_copy(T.off3[:, :], T.b3[:, 0:32]))
     wait("s", p_nt)
     s_nt = ev(S.activation(T.nt[:, :], T.b7[:, 256:257], AF.Copy))
 
-    wait("v", v_o3, s_k1)
+    wait("v", v_o3, s_k1, z_w1)
     v_w1 = ev(V.tensor_copy(T.W1[:, :].indirect(T.off3[:, :]), T.K1[:, :]))
-    m_w = ev(V.memset(T.Wm[:, 0:C], 0.0))
-    ev(V.memset(T.ATW[:, R:R + 8], 0), 1, m_w)
+    wait("v", s_mer, z_wm)
+    v_wm = ev(V.tensor_copy(T.Wm[:, :].indirect(T.off3[:, 0:16]), T.MeR[:, 0:256]))
     wait("p", v_w1, v_yy)
     for i in range(16):
         last = PE.matmul(T.b4[:, 0:96], T.YY[:, 15 - i:143 - i], T.W1[:, i:C:16], i == 0, i == 15)
@@ -258,70 +273,82 @@ def rank_program(g, core, T, topo):
     send("h2_%d" % q, lambda r: T.Lu[:, :], T.Lr[:, 96 * q:96 * q + 96])
     wait("g", s_nt)
     ev(g.dma_start(T.y[:, C:C + 1], T.nt[0:16, :], allow_slow_non_contiguous=True), 16)
+    wait("v", v_wm)
+    v_wm2 = ev(V.tensor_copy(T.Wm[:, :].indirect(T.off3[:, 16:32]), T.MeR[:, 256:512]))
 
-    wait("v", s_mer, m_w)
-    v_wm = ev(V.tensor_copy(T.Wm[:, :].indirect(T.off3[:, :]), T.MeR[:, :]))
-    wait("p", v_wm, s_nt)
-    p_m = new()
-    for c in range(12):
-        o = T.b7[:, c:128:8] if c < 8 else T.b7[:, 128 + c - 8:192:4]
-        ev(PE.matmul(o, T.Wm[:, 128 * c:128 * c + 128], T.onesb[:, 0:16], True, True), 1, p_m)
-
-    v_o2 = new()
-    order = [q] + [T.rank_of(c) for c in dests]
+    wait("v", v_lu)
+    v_o2 = ev(V.tensor_copy(T.off2[32 * q:32 * q + 32, :], T.Lu[32 * q:32 * q + 32, :]))
     for r in order:
-        if r == q:
-            wait("v", v_lu)
-            src = T.Lu[32 * q:32 * q + 32, :]
-        else:
-            total["h2_%d" % r] = 4
-            wait("v", "h2_%d" % r)
-            src = T.Lr[32 * q:32 * q + 32, 96 * r:96 * r + 96]
-        ev(V.tensor_copy(T.off2[32 * r:32 * r + 32, :], src), 1, v_o2)
-    wait("v", v_o2, d_at)
-    pc = {}
+        wait("v", "h2_%d" % r)
+        ev(V.tensor_copy(T.off2[32 * r:32 * r + 32, :], T.Lr[32 * q:32 * q + 32, 96 * r:96 * r + 96]), 1, v_o2)
+    wait("v", v_o2, d_at, m_w)
     wait("p", c_sel)
-    for c in range(12):
+    pa, pb = new(), [new(), new()]
+    for c in range(8):
         e = ev(V.tensor_copy(T.G[:, 128 * c:128 * c + 128], T.ATW[:, :].indirect(T.off2[:, 8 * c:8 * c + 8])))
         wait("p", e)
-        o = T.b5[:, c:512:8] if c < 8 else T.b6[:, c - 8:256:4]
-        m = PE.matmul(o, T.G[:, 128 * c:128 * c + 128], T.sele[:, :], True, True)
-        if c in (0, 8):
-            pc[c // 8] = new()
-        ev(m, 1, pc[c // 8])
-        if c == 7:
-            wait("s", pc[0])
-            s_sa = ev(S.activation(T.SA[:, :], T.b5[:, :], AF.Copy))
-            wait("g", s_sa)
-            send("h3a_%d" % q, lambda r: T.SA[:, 128 * r:128 * r + 128], T.LA[:, 128 * q:128 * q + 128])
-    wait("v", pc[1])
-    v_sb = ev(V.tensor_copy(T.SB[:, :], T.b6[:, 0:256]))
-    wait("g", v_sb)
-    send("h3b_%d" % q, lambda r: T.SB[:, 64 * r:64 * r + 64], T.LB[:, 64 * q:64 * q + 64])
+        ev(PE.matmul(T.b5[:, c:512:8], T.G[:, 128 * c:128 * c + 128], T.sele[:, :], True, True), 1, pa)
+    for c in (8, 10):
+        e = ev(V.tensor_copy(T.G[:, 128 * c:128 * c + 256], T.ATW[:, :].indirect(T.off2[:, 8 * c:8 * c + 16])))
+        wait("p", e)
+        for ch in range(2):
+            k = c // 2 - 4
+            ev(PE.matmul((T.b6 if ch == 0 else T.b2)[:, k:128:2], T.G[:, 128 * c + ch:128 * c + 256:2], T.sele[:, :],
+                         True, True), 1, pb[ch])
+    wait("s", pa)
+    s_sa = ev(S.activation(T.SA[:, :], T.b5[:, :], AF.Copy))
+    wait("g", s_sa)
+    send("h3a_%d" % q, lambda r: T.SA[:, 128 * r:128 * r + 128], T.LA[:, 128 * q:128 * q + 128])
+    wait("p", v_wm2, s_nt)
+    p_m = new()
+    for c in range(12):
+        o = T.b7[:, c:128:8]
+        l = T.Wm[:, 128 * c:128 * c + 128]
+        if c >= 8:
+            k, ch = (c - 8) // 2, c % 2
+            o = T.b7[:, 128 + 32 * ch + k:160 + 32 * ch:2]
+            l = T.Wm[:, 1024 + 256 * k + ch:1280 + 256 * k:2]
+        ev(PE.matmul(o, l, T.onesb[:, 0:16], True, True), 1, p_m)
+    SB, LB, ps_b = [T.SB0, T.SB1], [T.LB0, T.LB1], [T.b6, T.b2]
+    v_sb = []
+    for ch in range(2):
+        wait("v", pb[ch])
+        v_sb.append(ev(V.transpose(SB[ch][:, :], ps_b[ch][:, 0:128])))
+        wait("g", v_sb[ch])
+        b = SB[ch]
+        send("h3b%d_%d" % (ch, q), lambda r: b[:, 32 * r:32 * r + 32], LB[ch][:, 32 * q:32 * q + 32])
 
-    wait("v", s_sa, v_sb, p_m)
-    a = ev(V.tensor_tensor(T.accA[:, :], T.SA[:, 128 * q:128 * q + 128], T.b7[:, 0:128], A.add))
-    b = ev(V.tensor_tensor(T.accB[:, :], T.SB[:, 64 * q:64 * q + 64], T.b7[:, 128:192], A.add))
-    for r in order[1:]:
-        total["h3a_%d" % r] = 4
+    mA = T.b7[:, 0:128]
+    wait("v", p_m)
+    t = ev(V.transpose(T.tB[:, :], T.b7[:, 128:192]))
+    wait("v", s_sa)
+    a = ev(V.tensor_tensor(mA, mA, T.SA[:, 128 * q:128 * q + 128], A.add))
+    x = []
+    wait("v", t, *v_sb)
+    for ch in range(2):
+        o = T.tB[:, 32 * ch:32 * ch + 32]
+        x.append(ev(V.tensor_tensor(o, o, SB[ch][:, 32 * q:32 * q + 32], A.add)))
+    for r in order:
         wait("v", "h3a_%d" % r, a)
-        a = ev(V.tensor_tensor(T.accA[:, :], T.accA[:, :], T.LA[:, 128 * r:128 * r + 128], A.add))
+        o = T.accA[:, :] if r == order[-1] else mA
+        a = ev(V.tensor_tensor(o, mA, T.LA[:, 128 * r:128 * r + 128], A.add))
     wait("p", a, c_idf)
     p_a = ev(PE.matmul(T.b0[:, 0:128], T.accA[:, :], T.idf[:, :], True, True))
     wait("s", p_a)
     s_oa = ev(S.activation(T.OA[:, :], T.b0[:, 0:128], AF.Copy))
     wait("y", s_oa)
     ev(SY.dma_start(T.y[:, 0:1024], T.OA[:, :]), 16)
-    for r in order[1:]:
-        total["h3b_%d" % r] = 4
-        wait("v", "h3b_%d" % r, b)
-        b = ev(V.tensor_tensor(T.accB[:, :], T.accB[:, :], T.LB[:, 64 * r:64 * r + 64], A.add))
-    wait("p", b)
-    p_b = ev(PE.matmul(T.b1[0:64, 0:128], T.accB[:, :], T.idf[:, :], True, True))
-    wait("v", p_b)
-    v_ob = ev(V.tensor_copy(T.OB[0:64, :], T.b1[0:64, 0:128]))
-    wait("s", v_ob)
-    ev(S.dma_start(T.y[:, 1024:1536], T.OB[0:64, :]), 16)
+    for r in order:
+        for ch in range(2):
+            wait("v", "h3b%d_%d" % (ch, r), x[ch])
+            i = T.tB[:, 32 * ch:32 * ch + 32]
+            o = T.OB[:, ch:64:2] if r == order[-1] else i
+            x[ch] = ev(V.tensor_tensor(o, i, LB[ch][:, 32 * r:32 * r + 32], A.add))
+    for n, k in (("y", 0), ("s", 1)):
+        wait(n, *x)
+        for b in range(4):
+            ev(queues[n].dma_start(T.y[:, 1024 + 256 * k + 64 * b:1088 + 256 * k + 64 * b],
+                                   T.OB[32 * b + k:32 * b + 32:2, :]), 16)
 
     for s in total:
         if waited.get(s, 0) < total[s]:

from concourse.bass import DstId, RemoteDMATransfer
from concourse.mybir import AluOpType as A, ActivationFunctionType as AF
import numpy as np

R, F, C, D, NR = 8192, 4096, 1536, 2, 4
TR = 3584
EARLY = 2
P1, P2 = 2560, 4608

SCRATCH = {
    "limi": ("sbuf", [128, 2], "int32"), "limf": ("sbuf", [128, 2], "float32"),
    "a0": ("sbuf", [128, 128], "int32"), "ps": ("sbuf", [128, 128], "bfloat16"),
    "PD": ("dram", [NR, 128, 128], "bfloat16"),
    "pw": ("sbuf", [128, R], "bfloat16"), "Pg": ("sbuf", [128, F], "bfloat16"),
    "fkt": ("sbuf", [128, 256], "int32"), "off16": ("sbuf", [128, 256], "uint16"),
    "fhi": ("sbuf", [128, 256], "int32"), "flo": ("sbuf", [128, 256], "int32"),
    "fhib": ("sbuf", [128, 256], "bfloat16"), "flob": ("sbuf", [128, 256], "bfloat16"),
    "K1": ("sbuf", [128, 512], "bfloat16"), "W1": ("sbuf", [128, TR], "bfloat16"),
    "mei": ("sbuf", [128, 32], "int32"), "mep": ("sbuf", [128, 96], "int32"),
    "MEL": ("sbuf", [128, 512], "bfloat16"), "MeR": ("sbuf", [128, 512], "bfloat16"),
    "Wm": ("sbuf", [128, TR], "bfloat16"),
    "onesb": ("sbuf", [128, 128], "bfloat16"), "onesf": ("sbuf", [128, 128], "float32"),
    "zb": ("sbuf", [128, 128], "bfloat16"),
    "limsel": ("sbuf", [128, 128], "float32"), "Qt": ("sbuf", [128, 260], "bfloat16"),
    "YY": ("sbuf", [128, 144], "bfloat16"), "kc": ("sbuf", [128, 1], "int32"),
    "kx": ("sbuf", [128, 1], "int32"), "kxf": ("sbuf", [128, 1], "float32"),
    "ku": ("sbuf", [128, 1], "int32"), "kuf": ("sbuf", [128, 1], "float32"),
    "row2d": ("sbuf", [128, 8], "float32"), "rowj": ("sbuf", [128, 32], "float32"),
    "J": ("sbuf", [128, 32], "float16"),
    "mats": ("sbuf", [128, 384], "bfloat16"), "H": ("sbuf", [128, 640], "float16"),
    "idb": ("sbuf", [128, 128], "bfloat16"), "idf": ("sbuf", [128, 128], "float32"),
    "sele": ("sbuf", [128, 64], "float32"),
    "Msk": ("sbuf", [128, 32], "float16"), "Sc": ("sbuf", [128, 16], "float16"),
    "MJ": ("sbuf", [128, 32], "float16"), "off3": ("sbuf", [128, 32], "uint16"),
    "nt": ("sbuf", [128, 1], "float32"),
    "Lu": ("sbuf", [128, 96], "uint16"), "Lr": ("sbuf", [128, NR * 96], "uint16"),
    "off2": ("sbuf", [128, 96], "uint16"),
    "ATW": ("sbuf", [128, R + 8], "int32"), "G": ("sbuf", [128, C], "float32"),
    "SA": ("sbuf", [128, 512], "float32"), "LA": ("sbuf", [128, 512], "float32"),
    "SB0": ("sbuf", [128, 128], "float32"), "LB0": ("sbuf", [128, 128], "float32"),
    "SB1": ("sbuf", [128, 128], "float32"), "LB1": ("sbuf", [128, 128], "float32"),
    "accA": ("sbuf", [128, 128], "float32"), "tB": ("sbuf", [128, 64], "float32"),
    "OA": ("sbuf", [128, 128], "float32"), "OB": ("sbuf", [128, 64], "float32"),
}
for _b in range(8):
    SCRATCH["b%d" % _b] = ("psum", [128, 512], "float32")
NEV = 122
SEMAPHORES = (["e%d" % _i for _i in range(NEV)] + ["left", "h1"]
              + ["%s_%d" % (_n, _q) for _n in ("h2", "h3a", "h3b0", "h3b1") for _q in range(NR)])


def rank_program(g, core, T, topo):
    q = T.rank_of(core)
    if q is None:
        return
    V, S, PE, SY = g.vector, g.scalar, g.tensor, g.sync
    queues = {"g": g, "v": V, "s": S, "p": PE, "y": SY}
    used, total, seen, waited = [0], {}, {}, {}

    def new():
        s = "e%d" % used[0]
        used[0] += 1
        return s

    def ev(inst, n=1, s=None):
        if s is None:
            s = new()
        inst.then_inc(T.sem[s], n)
        total[s] = total.get(s, 0) + n
        return s

    def wait(k, *names):
        for s in names:
            n = total[s]
            if seen.get((k, s), 0) < n:
                queues[k].wait_ge(T.sem[s], n)
                seen[(k, s)] = n
                waited[s] = max(waited.get(s, 0), n)

    others = [c for c in T.cores if c != core]
    cross = [c for c in others if topo.die(c) != topo.die(core)]
    same = [c for c in others if topo.die(c) == topo.die(core)]
    dests = cross[:1] + same + cross[1:]
    order = [T.rank_of(c) for c in dests]
    total["h1"] = 12
    for n in ("h2", "h3a", "h3b0", "h3b1"):
        for r in order:
            total["%s_%d" % (n, r)] = 4

    def send(rsem, src, dst):
        tr = []
        for k, c in enumerate(dests):
            rid, pid, _ = topo.addr(c)
            mask = sum(1 << e for e in topo.engines(core, c)[k::4])
            tr.append(RemoteDMATransfer(dst_ids=[DstId(rid=rid, pnc=pid)], dma_engine_mask=mask,
                                        remote_sem=T.sem[rsem], src=src(T.rank_of(c)), dst=dst))
        g.remote_dma_fused(tr, local_sem=T.sem.left)
        total["left"] = total.get("left", 0) + 4 * len(dests)

    def at_load(k):
        r, e = k // 2, k % 2
        p = 32 * r + 16 * e
        return SY.dma_start(T.ATW[p:p + 16, 0:R], T.at[:, R * e:R * e + R])

    d_lim = ev(SY.dma_start(T.limi[0:2, :], T.lim[0:1, :]), 16)
    d_a0 = ev(S.dma_start(T.a0[:, :], T.at[0:1, :]), 16)
    d_fk = ev(S.dma_start(T.fkt[:, :], T.fk[:, :]), 16)
    d_me = ev(SY.dma_start(T.mei[:, 0:16], T.me[0:1, 0:2048]), 16)
    ev(SY.dma_start(T.mei[:, 16:32], T.me[0:1, 2048:4096]), 16, d_me)
    d_at = new()
    for k in range(EARLY):
        ev(at_load(k), 16, d_at)

    z0 = ev(V.memset(T.pw[:, 0:1024], 0.0))
    m_one = ev(V.memset(T.onesf[:, :], 1.0))
    ev(V.memset(T.onesb[:, :], 1.0), 1, m_one)
    m_z = ev(V.memset(T.zb[:, :], 0.0))
    ev(V.memset(T.Qt[:, :], 0.0), 1, m_z)
    z1 = ev(V.memset(T.pw[:, 1024:P1], 0.0))
    wait("s", z0)
    z2 = new()
    for k in range(P2, R, 1024):
        n = min(1024, R - k)
        ev(S.activation(T.pw[:, k:k + n], T.pw[:, 0:n], AF.Copy), 1, z2)

    wait("g", m_one)
    c_lim = ev(g.affine_select(T.limsel[0:2, :], T.onesf[0:2, :], [[1, 2], [0, 64]], A.is_equal, 0.0, 0, -1))
    wait("g", m_z)
    c_q = new()
    for h in range(2):
        ev(g.affine_select(T.Qt[:, 130 * h + 1:130 * h + 129:2], T.onesb[:, 0:64], [[2, 8], [16, 8]],
                           A.is_equal, 0.0, h, -1), 1, c_q)
    c_io = ev(g.iota(T.kc[:, :], [[0, 1]], 0, 1))
    ev(g.iota(T.row2d[:, :], [[2, 8]], 0, 0, allow_small_or_imprecise_dtypes=True), 1, c_io)
    ev(g.iota(T.rowj[:, :], [[1, 2], [32, 16]], C, 0, allow_small_or_imprecise_dtypes=True), 1, c_io)

    wait("v", d_lim)
    v_lim = ev(V.tensor_copy(T.limf[0:2, :], T.limi[0:2, :]))
    wait("p", v_lim, c_lim)
    p_lim = ev(PE.matmul(T.b2[:, 480:482], T.limsel[0:2, :], T.limf[0:2, :], True, True))
    wait("v", d_a0, p_lim)
    v_cl = ev(V.tensor_scalar(out=T.b2[:, 128:256], in0=T.a0[:, :], scalar1=T.b2[:, 480:481],
                              scalar2=T.b2[:, 481:482], op0=A.max, op1=A.min))
    wait("v", v_cl)
    v_ps = ev(V.tensor_tensor(T.ps[:, :], T.b2[:, 128:256], T.a0[:, :], A.is_equal))
    wait("g", v_ps)
    send("h1", lambda r: T.ps[:, :], T.PD[q])
    ev(V.memset(T.pw[:, P1:P2], 0.0), 1, z1)
    wait("y", v_ps, z0, z1, z2)
    d_pw = ev(SY.dma_start(T.pw[32 * q:32 * q + 32:16, :], T.ps[:, :]), 16)
    wait("y", "h1")
    for lo, hi in ((0, q), (q + 1, NR)):
        if lo < hi:
            ev(SY.dma_start(T.pw[32 * lo:32 * hi:16, :], T.PD[lo:hi]), 16, d_pw)
    for k in range(EARLY, 8):
        ev(at_load(k), 16, d_at)

    wait("v", d_fk)
    v_off = ev(V.tensor_copy(T.off16[:, :], T.fkt[:, :]))
    v_k = ev(V.tensor_scalar(out=T.fhi[:, :], in0=T.fkt[:, :], scalar1=0x1F80, scalar2=None, op0=A.bitwise_and))
    ev(V.tensor_scalar(out=T.flo[:, :], in0=T.fkt[:, :], scalar1=127, scalar2=None, op0=A.bitwise_and), 1, v_k)
    wait("v", v_k)
    v_kb = ev(V.tensor_scalar(out=T.fhib[:, :], in0=T.fhi[:, :], scalar1=-8192.0, scalar2=None, op0=A.add))
    ev(V.tensor_copy(T.flob[:, :], T.flo[:, :]), 1, v_kb)
    wait("p", v_kb, c_q)
    p_r = new()
    for h in range(2):
        o = T.b0[:, 256 * h:256 * h + 256]
        ev(PE.matmul(o, T.Qt[:, 130 * h + 1:130 * h + 129], T.fhib[:, :], True, False), 1, p_r)
        ev(PE.matmul(o, T.Qt[:, 130 * h:130 * h + 128], T.flob[:, :], False, True), 1, p_r)
    wait("s", p_r)
    s_k1 = ev(S.activation(T.K1[:, :], T.b0[:, :], AF.Copy))

    c_idb = ev(g.affine_select(T.idb[:, :], T.onesb[:, :], [[1, 128]], A.is_equal, 0.0, 0, -1))
    c_m = new()
    pat = [[1, 8], [8, 16]]
    ev(g.affine_select(T.mats[:, 0:128], T.zb[:, :], pat, A.is_gt, -1.0, 0, -1), 1, c_m)
    ev(g.affine_select(T.mats[:, 128:256], T.zb[:, :], pat, A.is_ge, -1.0, 0, -1), 1, c_m)
    ev(g.affine_select(T.mats[:, 256:384], T.onesb[:, :], pat, A.is_equal, 0.0, 0, -1), 1, c_m)
    z_w1 = ev(g.iota(T.W1[:, 0:C], [[0, C]], 0, 0, allow_small_or_imprecise_dtypes=True))
    c_s1 = ev(g.affine_select(T.sele[:, :], T.onesf[:, 0:64], [[32, 4], [1, 16]], A.is_equal, 0.0, 0, -1))
    c_idf = ev(g.affine_select(T.idf[:, :], T.onesf[:, :], [[1, 128]], A.is_equal, 0.0, 0, -1))
    wait("g", c_s1)
    c_sel = ev(g.affine_select(T.sele[:, :], T.sele[:, :], [[32, 4], [1, 16]], A.not_equal, 1.0, 16, -1))

    m_w = ev(V.memset(T.ATW[:, R:R + 8], 0))
    m_mel = ev(V.memset(T.MEL[:, :], 0.0))
    wait("v", d_me, c_io)
    v_mp = ev(V.tensor_scalar(out=T.mep[:, 0:32], in0=T.mei[:, :], scalar1=14, scalar2=None, op0=A.arith_shift_right))
    ev(V.tensor_scalar(out=T.mep[:, 32:64], in0=T.mei[:, :], scalar1=0x3F80, scalar2=None, op0=A.bitwise_and), 1, v_mp)
    ev(V.tensor_scalar(out=T.mep[:, 64:96], in0=T.mei[:, :], scalar1=127, scalar2=None, op0=A.bitwise_and), 1, v_mp)
    v_ku = ev(V.tensor_scalar(out=T.ku[:, :], in0=T.kc[:, :], scalar1=3, scalar2=None, op0=A.arith_shift_right))
    v_kx = ev(V.tensor_scalar(out=T.kx[:, :], in0=T.kc[:, :], scalar1=14, scalar2=None, op0=A.bitwise_and))
    wait("v", v_mp, m_mel)
    v_mel = new()
    for x in range(3):
        for h in range(2):
            ev(V.tensor_scalar(out=T.MEL[:, 256 * h + x:256 * h + 256:16], in0=T.mep[:, 32 * x + h:32 * x + 32:2],
                               scalar1=16384.0 if x == 0 else 1.0, scalar2=None, op0=A.mult), 1, v_mel)
    wait("v", v_ku)
    v_kf = ev(V.tensor_scalar(out=T.kuf[:, :], in0=T.ku[:, :], scalar1=2.0, scalar2=None, op0=A.mult))
    wait("p", v_mel, c_idb)
    p_me = new()
    for x in range(4):
        ev(PE.matmul(T.b1[:, 128 * x:128 * x + 128], T.MEL[:, 128 * x:128 * x + 128], T.idb[:, :], True, True), 1, p_me)

    wait("v", d_pw, v_off, z0, z1)
    wait("s", d_pw, v_off, z0, z1)
    p_c = new()
    vgot = []
    for lo, hi in ((0, 3), (3, 5), (5, 7), (7, 8)):
        got = [ev(V.tensor_copy(T.Pg[:, 256 * lo:256 * hi], T.pw[:, :].indirect(T.off16[:, 16 * lo:16 * hi]))),
               ev(S.activation(T.Pg[:, 2048 + 256 * lo:2048 + 256 * hi],
                               T.pw[:, :].indirect(T.off16[:, 128 + 16 * lo:128 + 16 * hi]), AF.Copy))]
        vgot.append(got[0])
        for b in range(2):
            wait("p", got[b])
            for uh in range(8 * b + lo, 8 * b + hi):
                for h in range(2):
                    w = 16 * h + uh
                    ev(PE.matmul(T.b2[:, w:w + 1], T.Pg[:, 256 * uh + h:256 * uh + 256:2], T.onesb[:, 0:1], True, True),
                       1, p_c)
    wait("s", p_me)
    s_mer = ev(S.activation(T.MeR[:, :], T.b1[:, :], AF.Copy))
    wait("s", *vgot)
    z_wm = ev(S.activation(T.Wm[:, 0:C], T.Pg[:, 0:C], AF.Copy, scale=0.0))

    wait("v", c_m, v_kf)
    v_h = ev(V.tensor_copy(T.H[:, 0:384], T.mats[:, :]))
    v_j = ev(V.tensor_scalar(out=T.J[:, :], in0=T.rowj[:, :], scalar1=T.kuf[:, :], scalar2=None, op0=A.add))
    ev(V.tensor_copy(T.H[:, 512:640], T.onesb[:, :]), 1, v_h)
    ev(V.tensor_scalar(out=T.H[:, 384:512], in0=T.mats[:, 256:384], scalar1=-1.0, scalar2=None, op0=A.mult), 1, v_h)
    L1, L1B, IP, NIP, ONE = [T.H[:, 128 * k:128 * k + 128] for k in range(5)]
    wait("p", v_h, v_j)
    PE.matmul(T.b3[:, 0:32], IP, T.J[:, :], True, False)
    wait("v", p_c)
    v_m = ev(V.tensor_scalar(out=T.Msk[:, :], in0=T.b2[:, 0:32], scalar1=7.5, scalar2=None, op0=A.is_gt))
    wait("v", v_m)
    v_sc = ev(V.tensor_tensor_scan(T.Sc[:, :], T.Msk[:, 0:16], T.Msk[:, 16:32], 0.0, A.add, A.add))
    v_mj = ev(V.tensor_tensor(T.MJ[:, :], T.Msk[:, :], T.J[:, :], A.mult))
    wait("p", v_m)
    PE.matmul(T.b3[:, 0:32], L1, T.Msk[:, :], False, False)
    PE.matmul(T.b3[:, 0:16], L1, T.Msk[:, 16:32], False, False)
    PE.matmul(T.b3[:, 16:32], L1B, T.Msk[:, 0:16], False, False)
    wait("p", v_sc)
    PE.matmul(T.b3[:, 0:16], ONE, T.Sc[:, :], False, False)
    PE.matmul(T.b3[:, 16:32], ONE, T.Sc[:, :], False, False)
    wait("p", v_mj)
    p_pos = ev(PE.matmul(T.b3[:, 0:32], NIP, T.MJ[:, :], False, True))
    p_nt = ev(PE.matmul(T.b7[:, 256:257], ONE, T.Sc[:, 15:16], True, True))
    wait("v", v_kx)
    v_kf2 = ev(V.tensor_copy(T.kxf[:, :], T.kx[:, :]))
    m_yy = ev(V.memset(T.YY[:, :], 0.0))
    wait("v", v_kf2, m_yy)
    v_yy = ev(V.tensor_scalar(out=T.YY[:, 15:143:16], in0=T.row2d[:, :], scalar1=T.kxf[:, :], scalar2=None,
                              op0=A.is_equal))
    wait("v", p_pos)
    v_o3 = ev(V.tensor_copy(T.off3[:, :], T.b3[:, 0:32]))
    wait("s", p_nt)
    s_nt = ev(S.activation(T.nt[:, :], T.b7[:, 256:257], AF.Copy))

    wait("v", v_o3, s_k1, z_w1)
    v_w1 = ev(V.tensor_copy(T.W1[:, :].indirect(T.off3[:, :]), T.K1[:, :]))
    wait("v", s_mer, z_wm)
    v_wm = ev(V.tensor_copy(T.Wm[:, :].indirect(T.off3[:, 0:16]), T.MeR[:, 0:256]))
    wait("p", v_w1, v_yy)
    for i in range(16):
        last = PE.matmul(T.b4[:, 0:96], T.YY[:, 15 - i:143 - i], T.W1[:, i:C:16], i == 0, i == 15)
    p_l = ev(last)
    wait("v", p_l)
    v_lu = ev(V.tensor_scalar(out=T.Lu[:, :], in0=T.b4[:, 0:96], scalar1=8192.0, scalar2=None, op0=A.add))
    wait("g", v_lu)
    send("h2_%d" % q, lambda r: T.Lu[:, :], T.Lr[:, 96 * q:96 * q + 96])
    wait("g", s_nt)
    ev(g.dma_start(T.y[:, C:C + 1], T.nt[0:16, :], allow_slow_non_contiguous=True), 16)
    wait("v", v_wm)
    v_wm2 = ev(V.tensor_copy(T.Wm[:, :].indirect(T.off3[:, 16:32]), T.MeR[:, 256:512]))

    wait("v", v_lu)
    v_o2 = ev(V.tensor_copy(T.off2[32 * q:32 * q + 32, :], T.Lu[32 * q:32 * q + 32, :]))
    for r in order:
        wait("v", "h2_%d" % r)
        ev(V.tensor_copy(T.off2[32 * r:32 * r + 32, :], T.Lr[32 * q:32 * q + 32, 96 * r:96 * r + 96]), 1, v_o2)
    wait("v", v_o2, d_at, m_w)
    wait("p", c_sel)
    pa, pb = new(), [new(), new()]
    for c in range(8):
        e = ev(V.tensor_copy(T.G[:, 128 * c:128 * c + 128], T.ATW[:, :].indirect(T.off2[:, 8 * c:8 * c + 8])))
        wait("p", e)
        ev(PE.matmul(T.b5[:, c:512:8], T.G[:, 128 * c:128 * c + 128], T.sele[:, :], True, True), 1, pa)
    for c in (8, 10):
        e = ev(V.tensor_copy(T.G[:, 128 * c:128 * c + 256], T.ATW[:, :].indirect(T.off2[:, 8 * c:8 * c + 16])))
        wait("p", e)
        for ch in range(2):
            k = c // 2 - 4
            ev(PE.matmul((T.b6 if ch == 0 else T.b2)[:, k:128:2], T.G[:, 128 * c + ch:128 * c + 256:2], T.sele[:, :],
                         True, True), 1, pb[ch])
    wait("s", pa)
    s_sa = ev(S.activation(T.SA[:, :], T.b5[:, :], AF.Copy))
    wait("g", s_sa)
    send("h3a_%d" % q, lambda r: T.SA[:, 128 * r:128 * r + 128], T.LA[:, 128 * q:128 * q + 128])
    wait("p", v_wm2, s_nt)
    p_m = new()
    for c in range(12):
        o = T.b7[:, c:128:8]
        l = T.Wm[:, 128 * c:128 * c + 128]
        if c >= 8:
            k, ch = (c - 8) // 2, c % 2
            o = T.b7[:, 128 + 32 * ch + k:160 + 32 * ch:2]
            l = T.Wm[:, 1024 + 256 * k + ch:1280 + 256 * k:2]
        ev(PE.matmul(o, l, T.onesb[:, 0:16], True, True), 1, p_m)
    SB, LB, ps_b = [T.SB0, T.SB1], [T.LB0, T.LB1], [T.b6, T.b2]
    v_sb = []
    for ch in range(2):
        wait("v", pb[ch])
        v_sb.append(ev(V.transpose(SB[ch][:, :], ps_b[ch][:, 0:128])))
        wait("g", v_sb[ch])
        b = SB[ch]
        send("h3b%d_%d" % (ch, q), lambda r: b[:, 32 * r:32 * r + 32], LB[ch][:, 32 * q:32 * q + 32])

    mA = T.b7[:, 0:128]
    wait("v", p_m)
    t = ev(V.transpose(T.tB[:, :], T.b7[:, 128:192]))
    wait("v", s_sa)
    a = ev(V.tensor_tensor(mA, mA, T.SA[:, 128 * q:128 * q + 128], A.add))
    x = []
    wait("v", t, *v_sb)
    for ch in range(2):
        o = T.tB[:, 32 * ch:32 * ch + 32]
        x.append(ev(V.tensor_tensor(o, o, SB[ch][:, 32 * q:32 * q + 32], A.add)))
    for r in order:
        wait("v", "h3a_%d" % r, a)
        o = T.accA[:, :] if r == order[-1] else mA
        a = ev(V.tensor_tensor(o, mA, T.LA[:, 128 * r:128 * r + 128], A.add))
    wait("p", a, c_idf)
    p_a = ev(PE.matmul(T.b0[:, 0:128], T.accA[:, :], T.idf[:, :], True, True))
    wait("s", p_a)
    s_oa = ev(S.activation(T.OA[:, :], T.b0[:, 0:128], AF.Copy))
    wait("y", s_oa)
    ev(SY.dma_start(T.y[:, 0:1024], T.OA[:, :]), 16)
    for r in order:
        for ch in range(2):
            wait("v", "h3b%d_%d" % (ch, r), x[ch])
            i = T.tB[:, 32 * ch:32 * ch + 32]
            o = T.OB[:, ch:64:2] if r == order[-1] else i
            x[ch] = ev(V.tensor_tensor(o, i, LB[ch][:, 32 * r:32 * r + 32], A.add))
    for n, k in (("y", 0), ("s", 1)):
        wait(n, *x)
        for b in range(4):
            ev(queues[n].dma_start(T.y[:, 1024 + 256 * k + 64 * b:1088 + 256 * k + 64 * b],
                                   T.OB[32 * b + k:32 * b + 32:2, :]), 16)

    for s in total:
        if waited.get(s, 0) < total[s]:
            wait("g", s)
